import numpy as np
import ml_dtypes


def mxq(x, axis, fmt="e4m3"):
    dtype, down = {"e4m3": (ml_dtypes.float8_e4m3fn, 7), "e5m2": (ml_dtypes.float8_e5m2, 14)}[fmt]
    v = np.moveaxis(np.asarray(x, np.float32).astype(ml_dtypes.bfloat16).astype(np.float64), axis, -1)
    blocks = v.reshape(v.shape[:-1] + (-1, 32))
    amax = np.abs(blocks).max(-1, keepdims=True)
    byte = np.maximum(np.where(amax > 0, np.frexp(amax)[1] - 1 + 127, 0) - down, 1)
    scale = np.exp2(byte - 127.0)
    codes = (blocks / scale).astype(np.float32).astype(dtype).astype(np.float64)
    return np.moveaxis((codes * scale).reshape(v.shape), -1, axis)


WIDE = False


def mx_kscale(k):
    if not WIDE:
        return np.ones(k)
    levels = np.array([10, -10, 5, -5, 0])
    if k % 512:
        return np.exp2(np.random.permutation(np.resize(levels, k // 32))).repeat(32)
    a = np.empty((k // 512, 16))
    for p in range(k // 512):
        a[p, :8] = np.random.permutation(np.resize(levels, 8))
        for g in range(8):
            far = levels[np.abs(levels - a[p, g]) >= 10]
            a[p, g + 8] = far[np.random.randint(len(far))]
    return np.exp2(a.ravel()).repeat(32)


def f64(x):
    return np.asarray(x).astype(np.float64)


def striped8(idx):
    return np.asarray(idx).reshape(8, -1, 16).transpose(0, 2, 1).reshape(128, -1).astype(np.uint16)


def unstriped8(offs):
    return offs.reshape(8, 16, -1).transpose(0, 2, 1).reshape(8, -1).astype(np.int64)


def pick8(x, idx, run):
    r = np.arange(len(x))
    return x[r[:, None], idx[r % (8 * run) // run]]


E2M1 = np.array([0.0, 0.5, 1.0, 1.5, 2.0, 3.0, 4.0, 6.0, -0.0, -0.5, -1.0, -1.5, -2.0, -3.0, -4.0, -6.0])


def pack_weight(w, fmt):
    k, n = w.shape
    w = f64(np.asarray(w, np.float32).astype(ml_dtypes.bfloat16)).reshape(k // 32, 32, n)
    amax = np.abs(w).max(1)
    if fmt == "e4m3":
        byte = np.frexp(amax)[1] - 1 + 127 - 7
    else:
        mant, ex = np.frexp(amax / 6.0)
        byte = np.where(mant > 0.5, ex, ex - 1) + 127
    byte = np.clip(np.where(amax > 0, byte, 1), 1, 254)
    scaled = (w * np.exp2(127.0 - byte)[:, None, :]).reshape(k, n).astype(np.float32)
    by_word = np.ascontiguousarray(scaled.reshape(k // 512, 128, 4, n).transpose(0, 1, 3, 2))
    if fmt == "e4m3":
        words = by_word.astype(ml_dtypes.float8_e4m3fn).view(np.uint8)
    else:
        c = by_word.astype(ml_dtypes.float4_e2m1fn).view(np.uint8) & 0xF
        words = (c[..., 0::2] | (c[..., 1::2] << 4)).reshape(k // 512, 128, 2 * n)
    return np.ascontiguousarray(words), np.ascontiguousarray(byte.astype(np.uint8).reshape(k // 512, 16, n))


def unpack_weight(words, scales, fmt):
    g, _, n = scales.shape
    words = np.ascontiguousarray(words).reshape(g, 128, n, -1)
    if fmt == "e4m3":
        vals = words.view(ml_dtypes.float8_e4m3fn).astype(np.float64)
    else:
        nib = np.empty((g, 128, n, 4), np.uint8)
        nib[..., 0::2] = words & 0xF
        nib[..., 1::2] = words >> 4
        vals = E2M1[nib]
    vals = vals * np.repeat(np.exp2(scales.astype(np.float64) - 127.0), 8, axis=1)[..., None]
    return vals.transpose(0, 1, 3, 2).reshape(g * 512, n)


D, V, Q, I = 512, 2048, 128, 512


def setup_inputs():
    n = np.random.standard_normal
    idx = np.stack([np.random.permutation(V)[:I] for _ in range(8)])
    fd = mx_kscale(D)
    vocp = pack_weight(n((D, V)) / fd[:, None], "e2m1")
    return {
        "hid": (n((D, Q)) * 1.0 / np.sqrt(D) * fd[:, None]).astype(np.float32),
        "voc_words": vocp[0],
        "voc_scales": vocp[1],
        "mult": (np.random.uniform(100.0, 300.0, (Q, 1))).astype(np.float32),
        "sw": (np.random.uniform(0.005, 0.02, (1, I))).astype(np.float32),
        "base": (0.3 * n((Q, V))).astype(np.float32),
        "offs": striped8(idx),
    }


def reference(hid, voc_words, voc_scales, mult, sw, base, offs):
    idx = unstriped8(offs)
    vocu = unpack_weight(voc_words, voc_scales, "e2m1")
    hidq = mxq(f64(hid), 0, "e4m3")
    a = hidq.T @ vocu
    m1 = np.max(a, axis=1, keepdims=True)
    p = np.exp(a - m1)
    z = np.sum(p, axis=1, keepdims=True)
    px = np.exp(pick8(a, idx, 16) - m1)
    u1 = px / z
    du1 = f64(sw) * (1.0 - u1 * f64(mult)) / u1 + f64(sw) * np.log(u1) * (-1.0) * f64(mult)
    dpx = du1 / z
    dz = np.sum(du1 * px / np.square(z) * (-1.0), axis=1, keepdims=True)
    e1 = dpx * px
    s1 = np.zeros((Q, V))
    s1[np.arange(Q)[:, None], idx[np.arange(Q) % 128 // 16]] = e1
    da = dz * p + s1
    hda = da * 64.0 * 2.0 * 64.0
    he1 = pick8(hda, idx, 16)
    hdz = np.sum(hda * p, axis=1, keepdims=True)
    hdpx = he1 * px
    hdu1 = hdz * (-1.0) / np.square(z) * px + hdpx / z
    hu1 = hdu1 / u1 * f64(sw) * (-1.0) * f64(mult) + hdu1 * f64(mult) * (-1.0) * f64(sw) / u1 - hdu1 * f64(sw) * (1.0 - u1 * f64(mult)) / np.square(u1)
    hpx = he1 * dpx + hdz * (-1.0) / np.square(z) * du1 + hu1 / z
    hz = np.sum(hdz * (-1.0) * du1 * px / np.square(np.square(z)) * (-1.0), axis=1, keepdims=True) * z * 2.0 + np.sum(hdpx * du1 / np.square(z) * (-1.0), axis=1, keepdims=True) + np.sum(hu1 * px / np.square(z) * (-1.0), axis=1, keepdims=True)
    hp = hda * dz + hz
    e51 = hpx * px
    s51 = np.zeros((Q, V))
    s51[np.arange(Q)[:, None], idx[np.arange(Q) % 128 // 16]] = e51
    ha = hp * p + s51
    y = ha + f64(base)
    return y

@@ -1,0 +1,244 @@
+import math
+from contextlib import ExitStack
+
+import concourse.mybir as mybir
+from concourse.masks import make_identity
+
+D, V, Q, I = 512, 2048, 128, 512
+FLOPS = 2 * D * V * Q
+
+F32 = mybir.dt.float32
+BF16 = mybir.dt.bfloat16
+I32 = mybir.dt.int32
+U32 = mybir.dt.uint32
+U16 = mybir.dt.uint16
+U8 = mybir.dt.uint8
+FP8X4 = mybir.dt.float8_e4m3fn_x4
+FP4X4 = mybir.dt.float4_e2m1fn_x4
+ALU = mybir.AluOpType
+ACT = mybir.ActivationFunctionType
+
+P = 128
+PACK = 4
+BANK = 512
+BANKS = V // BANK
+BLOCKS = BANK // P
+GAIN = 64.0 * 2.0 * 64.0
+LN2 = math.log(2.0)
+GUESS_SLOPE = -LN2 / 2.0**23
+GUESS_OFFSET = 88.0
+
+
+def tile_attend_gpfocal_heads_kernel(tc, hid, voc_words, voc_scales, mult, sw, base, offs, out):
+    nc = tc.nc
+    with ExitStack() as ctx:
+        sb = ctx.enter_context(tc.tile_pool(name="sb", bufs=1))
+        ps = ctx.enter_context(tc.psum_pool(name="ps", bufs=1))
+
+        def col(name, n=1):
+            return sb.tile([P, n], F32, name=name)
+
+        def listed(name):
+            return sb.tile([P, I], F32, name=name)
+
+        def bank_cols(b):
+            return slice(b * BANK, (b + 1) * BANK)
+
+        def block_cols(j):
+            return slice(j * P, (j + 1) * P)
+
+        hid_raw = sb.tile([P, PACK, Q], F32, name="hid_raw")
+        nc.sync.dma_start(out=hid_raw[:], in_=hid.rearrange("(p t) q -> p t q", t=PACK))
+        sw_cols = col("sw_cols", PACK)
+        nc.sync.dma_start(out=sw_cols[:], in_=sw.rearrange("o (p c) -> p (o c)", c=PACK))
+        voc_sc = sb.tile([P, V], U8, name="voc_sc", align_bytes=64)
+        for g in range(4):
+            nc.sync.dma_start(
+                out=voc_sc[32 * g : 32 * g + 4, :].bitcast(I32),
+                in_=voc_scales[0, 4 * g : 4 * g + 4, :].bitcast(I32),
+            )
+        voc_w = []
+        for h in range(2):
+            t = sb.tile([P, V], U8, name="voc_w%d" % h, align_bytes=64)
+            nc.sync.dma_start(out=t[:].bitcast(I32), in_=voc_words[0, :, h * V : (h + 1) * V].bitcast(I32))
+            voc_w.append(t)
+        offsets = sb.tile([P, I // 16], U16, name="offsets")
+        nc.sync.dma_start(offsets[:], offs)
+        mul_col = col("mul_col")
+        nc.sync.dma_start(out=mul_col[:], in_=mult)
+
+        placed = sb.tile([P, V], F32, name="placed")
+        nc.vector.memset(placed[:], 0.0)
+        ident = sb.tile([P, P], F32, name="ident")
+        make_identity(nc, ident[:])
+
+        hid_bf = sb.tile([P, Q, PACK], BF16, name="hid_bf", tag="hold", align_bytes=64)
+        nc.vector.tensor_copy(out=hid_bf[:], in_=hid_raw[:].rearrange("p t q -> p q t"))
+        hid_codes = sb.tile([P, Q], U32, name="hid_codes", align_bytes=64)
+        hid_sc = sb.tile([P, Q], U8, name="hid_sc", align_bytes=64)
+        nc.vector.quantize_mx(
+            out=hid_codes[:].bitcast(FP8X4), scales=hid_sc[:], in_=hid_bf[:].rearrange("p q t -> p (q t)")
+        )
+        base_sb = sb.tile([P, V], F32, name="base_sb", tag="hold", align_bytes=64)
+        nc.sync.dma_start(out=base_sb[:], in_=base)
+
+        sw_ps = ps.tile([P, BANK], F32, name="sw_ps", tag="turned3")
+        for c in range(PACK):
+            nc.tensor.transpose(sw_ps[:, block_cols(c)], sw_cols[:, c : c + 1].to_broadcast([P, P]), ident[:])
+        sw_gain = listed("sw_gain")
+        sw_sum = col("sw_sum")
+        nc.scalar.activation(
+            out=sw_gain[:].rearrange("q (p c) -> q p c", c=PACK),
+            in_=sw_ps[:].rearrange("q (c p) -> q p c", c=PACK),
+            func=ACT.Identity,
+            scale=GAIN,
+            accum_out=sw_sum[:],
+        )
+
+        neg_a = sb.tile([P, V], F32, name="neg_a")
+        p_sb = sb.tile([P, V], F32, name="p_sb")
+        neg_max = col("neg_max", BANKS)
+        z_part = col("z_part", BANKS)
+        for b in range(BANKS):
+            a_ps = ps.tile([P, BANK], F32, name="a_ps", tag="row%d" % b)
+            half, part = divmod(b, 2)
+            nc.tensor.matmul_mx(
+                out=a_ps[:],
+                lhsT=hid_codes[:].bitcast(FP8X4),
+                lhsT_scale=hid_sc[:],
+                rhs=voc_w[half][:, part * 2 * BANK : (part + 1) * 2 * BANK].bitcast(FP4X4),
+                rhs_scale=voc_sc[:, bank_cols(b)],
+                start=True,
+                stop=True,
+            )
+            nc.vector.tensor_scalar(
+                out=neg_a[:, bank_cols(b)], in0=a_ps[:], scalar1=-1.0, scalar2=None,
+                op0=ALU.mult, op1=ALU.min, accum_out=neg_max[:, b : b + 1],
+            )
+            nc.scalar.activation(
+                out=p_sb[:, bank_cols(b)], in_=neg_a[:, bank_cols(b)], func=ACT.Exp, scale=-1.0,
+                bias=neg_max[:, b : b + 1], accum_out=z_part[:, b : b + 1],
+            )
+        neg_m1 = col("neg_m1")
+        nc.vector.tensor_reduce(out=neg_m1[:], in_=neg_max[:], axis=mybir.AxisListType.X, op=ALU.min)
+        neg_ax = listed("neg_ax")
+        nc.vector.tensor_copy(out=neg_ax[:], in_=neg_a[:].indirect(offsets[:]))
+
+        rescale = col("rescale", BANKS)
+        nc.scalar.activation(out=rescale[:], in_=neg_max[:], func=ACT.Exp, scale=-1.0, bias=neg_m1[:])
+        px = listed("px")
+        nc.scalar.activation(out=px[:], in_=neg_ax[:], func=ACT.Exp, scale=-1.0, bias=neg_m1[:])
+
+        z = col("z")
+        z_terms = col("z_terms", BANKS)
+        nc.vector.scalar_tensor_tensor(
+            out=z_terms[:], in0=rescale[:], scalar=1.0, in1=z_part[:], op0=ALU.mult, op1=ALU.mult, accum_out=z[:]
+        )
+        inv_z = col("inv_z")
+        nc.vector.reciprocal(out=inv_z[:], in_=z[:])
+        neg_y0h = col("neg_y0h")
+        nc.vector.tensor_scalar(out=neg_y0h[:], in0=z[:].bitcast(I32), scalar1=GUESS_SLOPE, scalar2=GUESS_OFFSET - 0.5, op0=ALU.mult, op1=ALU.add)
+        neg_y0k = col("neg_y0k")
+        nc.vector.tensor_scalar(out=neg_y0k[:], in0=z[:].bitcast(I32), scalar1=GUESS_SLOPE, scalar2=GUESS_OFFSET + 1.5, op0=ALU.mult, op1=ALU.add)
+        mul_inv_z = col("mul_inv_z")
+        nc.vector.tensor_tensor(out=mul_inv_z[:], in0=inv_z[:], in1=mul_col[:], op=ALU.mult)
+        neg_k0 = col("neg_k0")
+        nc.vector.tensor_scalar(out=neg_k0[:], in0=neg_y0k[:], scalar1=neg_m1[:], scalar2=-1.0, op0=ALU.add, op1=ALU.mult)
+        neg_share = col("neg_share", BANKS)
+        nc.vector.tensor_scalar(out=neg_share[:], in0=rescale[:], scalar1=inv_z[:], scalar2=-1.0, op0=ALU.mult, op1=ALU.mult)
+
+        ex0 = col("ex0")
+        sq0 = col("sq0")
+        ex1 = sb.tile([P, 1], F32, name="ex1", tag="after_ln")
+        neg_k1 = col("neg_k1")
+        neg_shift = col("neg_shift")
+        nc.scalar.activation(out=ex0[:], in_=z[:].bitcast(U32), func=ACT.Exp, scale=GUESS_SLOPE, bias=GUESS_OFFSET)
+        nc.scalar.activation(out=sq0[:], in_=ex0[:], func=ACT.Square, scale=z[:], bias=-2.0)
+        nc.scalar.activation(out=ex1[:], in_=sq0[:], func=ACT.Exp, scale=0.5, bias=neg_y0h[:])
+        nc.scalar.activation(out=neg_k1[:], in_=sq0[:], func=ACT.Identity, scale=-0.5, bias=neg_k0[:])
+        nc.scalar.activation(out=neg_shift[:], in_=ex1[:], func=ACT.Identity, scale=z[:], bias=neg_k1[:])
+
+        w = listed("w")
+        nc.vector.scalar_tensor_tensor(out=w[:], in0=px[:], scalar=mul_inv_z[:], in1=sw_gain[:], op0=ALU.mult, op1=ALU.mult)
+        n1 = listed("n1")
+        n1_sum = col("n1_sum")
+        nc.vector.scalar_tensor_tensor(out=n1[:], in0=neg_ax[:], scalar=neg_shift[:], in1=w[:], op0=ALU.add, op1=ALU.mult, accum_out=n1_sum[:])
+        nc.vector.tensor_tensor(out=placed[:].indirect(offsets[:]), in0=n1[:], in1=sw_gain[:], op=ALU.add)
+
+        neg_p = sb.tile([P, V], F32, name="neg_p", tag="after_ln")
+        for b in range(BANKS):
+            nc.scalar.activation(out=neg_p[:, bank_cols(b)], in_=p_sb[:, bank_cols(b)], func=ACT.Copy, scale=neg_share[:, b : b + 1])
+        e1_sum = sb.tile([P, 1], F32, name="e1_sum", tag="after_hda")
+        nc.scalar.activation(out=e1_sum[:], in_=n1_sum[:], func=ACT.Identity, bias=sw_sum[:])
+        root_coef = col("root_coef")
+        nc.scalar.activation(out=root_coef[:], in_=e1_sum[:], func=ACT.Copy, scale=1.0 / math.sqrt(GAIN))
+        neg_e = col("neg_e")
+        nc.scalar.activation(out=neg_e[:], in_=e1_sum[:], func=ACT.Copy, scale=-1.0 / GAIN)
+
+        e1 = listed("e1")
+        nc.vector.tensor_tensor(out=e1[:], in0=n1[:], in1=sw_gain[:], op=ALU.add)
+        ue = listed("ue")
+        ue_sum = col("ue_sum")
+        nc.vector.scalar_tensor_tensor(out=ue[:], in0=px[:], scalar=inv_z[:], in1=e1[:], op0=ALU.mult, op1=ALU.mult, accum_out=ue_sum[:])
+
+        hda = sb.tile([P, V], F32, name="hda")
+        nc.vector.scalar_tensor_tensor(out=hda[:], in0=neg_p[:], scalar=e1_sum[:], in1=placed[:], op0=ALU.mult, op1=ALU.add)
+        f = sb.tile([P, I], F32, name="f", tag="after_hda")
+        nc.vector.tensor_tensor(out=f[:], in0=n1[:], in1=w[:], op=ALU.subtract)
+        he = listed("he")
+        nc.vector.tensor_scalar(out=he[:], in0=hda[:].indirect(offsets[:]), scalar1=1.0 / GAIN, scalar2=0.0, op0=ALU.mult, op1=ALU.add)
+
+        turned = []
+        for b in range(BANKS):
+            t_ps = ps.tile([P, BANK], F32, name="t_ps", tag="turned%d" % b)
+            turned.append(t_ps)
+            for j in range(BLOCKS):
+                nc.tensor.matmul(t_ps[:, block_cols(j)], base_sb[:, block_cols(b * BLOCKS + j)], ident[:], start=(j == 0), stop=False, is_transpose=True)
+
+        def add_turned(b, term, last):
+            for j in range(BLOCKS):
+                nc.tensor.matmul(turned[b][:, block_cols(j)], term[:, block_cols(j)], ident[:], start=False, stop=(last and j == BLOCKS - 1), is_transpose=True)
+
+        sq_sum = col("sq_sum")
+        unused_sq = sb.tile([P, V], BF16, name="unused_sq")
+        nc.scalar.activation(out=unused_sq[:], in_=neg_p[:], func=ACT.Square, scale=math.sqrt(GAIN), accum_out=sq_sum[:])
+        g = col("g")
+        nc.scalar.activation(out=g[:], in_=sq_sum[:], func=ACT.Identity, scale=neg_e[:], bias=ue_sum[:])
+        centre = col("centre")
+        nc.scalar.activation(out=centre[:], in_=g[:], func=ACT.Copy, scale=-0.5 / math.sqrt(GAIN))
+        g_small = col("g_small")
+        nc.scalar.activation(out=g_small[:], in_=g[:], func=ACT.Copy, scale=1.0 / GAIN)
+        for b in range(BANKS):
+            quad = sb.tile([P, BANK], F32, name="quad%d" % b)
+            nc.scalar.activation(out=quad[:], in_=neg_p[:, bank_cols(b)], func=ACT.Square, scale=root_coef[:], bias=centre[:])
+            add_turned(b, quad, False)
+        centre_sq = col("centre_sq")
+        nc.scalar.activation(out=centre_sq[:], in_=centre[:], func=ACT.Square)
+        cross = listed("cross")
+        nc.scalar.activation(out=cross[:], in_=ue[:], func=ACT.Copy, scale=neg_e[:])
+
+        e51 = listed("e51")
+        e51_sum = col("e51_sum")
+        nc.vector.scalar_tensor_tensor(out=e51[:], in0=he[:], scalar=g_small[:], in1=f[:], op0=ALU.subtract, op1=ALU.mult, accum_out=e51_sum[:])
+        nc.vector.tensor_tensor(out=placed[:].indirect(offsets[:]), in0=e51[:], in1=cross[:], op=ALU.add)
+
+        def add_linear(b):
+            lin = sb.tile([P, BANK], F32, name="lin%d" % b)
+            nc.scalar.activation(out=lin[:], in_=neg_p[:, bank_cols(b)], func=ACT.Copy, scale=e51_sum[:])
+            add_turned(b, lin, True)
+
+        def finish(b):
+            dense_t = sb.tile([P, BANK], F32, name="dense_t%d" % b)
+            nc.scalar.copy(out=dense_t[:], in_=turned[b][:])
+            dense = ps.tile([P, BANK], F32, name="dense", tag="row%d" % b)
+            for j in range(BLOCKS):
+                nc.tensor.transpose(dense[:, block_cols(j)], dense_t[:, block_cols(j)], ident[:])
+            res = sb.tile([P, BANK], F32, name="res%d" % b)
+            nc.vector.scalar_tensor_tensor(out=res[:], in0=dense[:], scalar=centre_sq[:], in1=placed[:, bank_cols(b)], op0=ALU.subtract, op1=ALU.add)
+            nc.sync.dma_start(out=out[:, bank_cols(b)], in_=res[:])
+
+        add_linear(0)
+        for b in range(BANKS):
+            if b + 1 < BANKS:
+                add_linear(b + 1)
+            finish(b)

@@ -47,15 +47,15 @@ def tile_attend_gpfocal_heads_kernel(tc, hid, voc_words, voc_scales, mult, sw, b
         def block_cols(j):
             return slice(j * P, (j + 1) * P)
 
+        sw_cols = sb.tile([P, PACK], F32, name="sw_cols", tag="sw_first", align_bytes=64)
+        nc.sync.dma_start(out=sw_cols[:], in_=sw.rearrange("o (p c) -> p (o c)", c=PACK))
         hid_raw = sb.tile([P, PACK, Q], F32, name="hid_raw")
         nc.sync.dma_start(out=hid_raw[:], in_=hid.rearrange("(p t) q -> p t q", t=PACK))
-        sw_cols = col("sw_cols", PACK)
-        nc.sync.dma_start(out=sw_cols[:], in_=sw.rearrange("o (p c) -> p (o c)", c=PACK))
         voc_sc = sb.tile([P, V], U8, name="voc_sc", align_bytes=64)
         for g in range(4):
             nc.sync.dma_start(
-                out=voc_sc[32 * g : 32 * g + 4, :].bitcast(I32),
-                in_=voc_scales[0, 4 * g : 4 * g + 4, :].bitcast(I32),
+                out=voc_sc[g:P:32, :].bitcast(I32),
+                in_=voc_scales[0, g:16:4, :].bitcast(I32),
             )
         voc_w = []
         for h in range(2):
@@ -72,16 +72,6 @@ def tile_attend_gpfocal_heads_kernel(tc, hid, voc_words, voc_scales, mult, sw, b
         ident = sb.tile([P, P], F32, name="ident")
         make_identity(nc, ident[:])
 
-        hid_bf = sb.tile([P, Q, PACK], BF16, name="hid_bf", tag="hold", align_bytes=64)
-        nc.vector.tensor_copy(out=hid_bf[:], in_=hid_raw[:].rearrange("p t q -> p q t"))
-        hid_codes = sb.tile([P, Q], U32, name="hid_codes", align_bytes=64)
-        hid_sc = sb.tile([P, Q], U8, name="hid_sc", align_bytes=64)
-        nc.vector.quantize_mx(
-            out=hid_codes[:].bitcast(FP8X4), scales=hid_sc[:], in_=hid_bf[:].rearrange("p q t -> p (q t)")
-        )
-        base_sb = sb.tile([P, V], F32, name="base_sb", tag="hold", align_bytes=64)
-        nc.sync.dma_start(out=base_sb[:], in_=base)
-
         sw_ps = ps.tile([P, BANK], F32, name="sw_ps", tag="turned3")
         for c in range(PACK):
             nc.tensor.transpose(sw_ps[:, block_cols(c)], sw_cols[:, c : c + 1].to_broadcast([P, P]), ident[:])
@@ -95,9 +85,19 @@ def tile_attend_gpfocal_heads_kernel(tc, hid, voc_words, voc_scales, mult, sw, b
             accum_out=sw_sum[:],
         )
 
+        hid_bf = sb.tile([P, Q, PACK], BF16, name="hid_bf", tag="hold", align_bytes=64)
+        nc.vector.tensor_copy(out=hid_bf[:], in_=hid_raw[:].rearrange("p t q -> p q t"))
+        hid_codes = sb.tile([P, Q], U32, name="hid_codes", align_bytes=64)
+        hid_sc = sb.tile([P, Q], U8, name="hid_sc", tag="sw_first", align_bytes=64)
+        nc.vector.quantize_mx(
+            out=hid_codes[:].bitcast(FP8X4), scales=hid_sc[:], in_=hid_bf[:].rearrange("p q t -> p (q t)")
+        )
+        base_sb = sb.tile([P, V], F32, name="base_sb", tag="hold", align_bytes=64)
+        nc.sync.dma_start(out=base_sb[:], in_=base)
+
         neg_a = sb.tile([P, V], F32, name="neg_a")
         p_sb = sb.tile([P, V], F32, name="p_sb")
-        neg_max = col("neg_max", BANKS)
+        neg_max = sb.tile([P, BANKS], F32, name="neg_max", tag="after_max")
         z_part = col("z_part", BANKS)
         for b in range(BANKS):
             a_ps = ps.tile([P, BANK], F32, name="a_ps", tag="row%d" % b)
@@ -134,16 +134,21 @@ def tile_attend_gpfocal_heads_kernel(tc, hid, voc_words, voc_scales, mult, sw, b
         nc.vector.scalar_tensor_tensor(
             out=z_terms[:], in0=rescale[:], scalar=1.0, in1=z_part[:], op0=ALU.mult, op1=ALU.mult, accum_out=z[:]
         )
+        neg_mul = sb.tile([P, 2], F32, name="neg_mul", tag="after_max")
+        nc.vector.tensor_scalar(out=neg_mul[:, 0:1], in0=mul_col[:], scalar1=-1.0, scalar2=None, op0=ALU.mult)
+        nc.vector.tensor_scalar(out=neg_mul[:, 1:2], in0=mul_col[:], scalar1=-0.5, scalar2=None, op0=ALU.mult)
+        mul_ax = listed("mul_ax")
+        nc.vector.tensor_scalar(out=mul_ax[:], in0=neg_ax[:], scalar1=mul_col[:], scalar2=None, op0=ALU.mult)
         inv_z = col("inv_z")
         nc.vector.reciprocal(out=inv_z[:], in_=z[:])
         neg_y0h = col("neg_y0h")
         nc.vector.tensor_scalar(out=neg_y0h[:], in0=z[:].bitcast(I32), scalar1=GUESS_SLOPE, scalar2=GUESS_OFFSET - 0.5, op0=ALU.mult, op1=ALU.add)
         neg_y0k = col("neg_y0k")
         nc.vector.tensor_scalar(out=neg_y0k[:], in0=z[:].bitcast(I32), scalar1=GUESS_SLOPE, scalar2=GUESS_OFFSET + 1.5, op0=ALU.mult, op1=ALU.add)
-        mul_inv_z = col("mul_inv_z")
-        nc.vector.tensor_tensor(out=mul_inv_z[:], in0=inv_z[:], in1=mul_col[:], op=ALU.mult)
+        mul_z = col("mul_z")
+        nc.vector.tensor_tensor(out=mul_z[:], in0=z[:], in1=mul_col[:], op=ALU.mult)
         neg_k0 = col("neg_k0")
-        nc.vector.tensor_scalar(out=neg_k0[:], in0=neg_y0k[:], scalar1=neg_m1[:], scalar2=-1.0, op0=ALU.add, op1=ALU.mult)
+        nc.vector.tensor_scalar(out=neg_k0[:], in0=neg_y0k[:], scalar1=neg_m1[:], scalar2=neg_mul[:, 0:1], op0=ALU.add, op1=ALU.mult)
         neg_share = col("neg_share", BANKS)
         nc.vector.tensor_scalar(out=neg_share[:], in0=rescale[:], scalar1=inv_z[:], scalar2=-1.0, op0=ALU.mult, op1=ALU.mult)
 
@@ -155,36 +160,40 @@ def tile_attend_gpfocal_heads_kernel(tc, hid, voc_words, voc_scales, mult, sw, b
         nc.scalar.activation(out=ex0[:], in_=z[:].bitcast(U32), func=ACT.Exp, scale=GUESS_SLOPE, bias=GUESS_OFFSET)
         nc.scalar.activation(out=sq0[:], in_=ex0[:], func=ACT.Square, scale=z[:], bias=-2.0)
         nc.scalar.activation(out=ex1[:], in_=sq0[:], func=ACT.Exp, scale=0.5, bias=neg_y0h[:])
-        nc.scalar.activation(out=neg_k1[:], in_=sq0[:], func=ACT.Identity, scale=-0.5, bias=neg_k0[:])
-        nc.scalar.activation(out=neg_shift[:], in_=ex1[:], func=ACT.Identity, scale=z[:], bias=neg_k1[:])
+        nc.scalar.activation(out=neg_k1[:], in_=sq0[:], func=ACT.Identity, scale=neg_mul[:, 1:2], bias=neg_k0[:])
+        nc.scalar.activation(out=neg_shift[:], in_=ex1[:], func=ACT.Identity, scale=mul_z[:], bias=neg_k1[:])
 
         w = listed("w")
-        nc.vector.scalar_tensor_tensor(out=w[:], in0=px[:], scalar=mul_inv_z[:], in1=sw_gain[:], op0=ALU.mult, op1=ALU.mult)
+        w_sum = col("w_sum")
+        nc.vector.scalar_tensor_tensor(out=w[:], in0=px[:], scalar=inv_z[:], in1=sw_gain[:], op0=ALU.mult, op1=ALU.mult, accum_out=w_sum[:])
         n1 = listed("n1")
         n1_sum = col("n1_sum")
-        nc.vector.scalar_tensor_tensor(out=n1[:], in0=neg_ax[:], scalar=neg_shift[:], in1=w[:], op0=ALU.add, op1=ALU.mult, accum_out=n1_sum[:])
+        nc.vector.scalar_tensor_tensor(out=n1[:], in0=mul_ax[:], scalar=neg_shift[:], in1=w[:], op0=ALU.add, op1=ALU.mult, accum_out=n1_sum[:])
         nc.vector.tensor_tensor(out=placed[:].indirect(offsets[:]), in0=n1[:], in1=sw_gain[:], op=ALU.add)
 
-        neg_p = sb.tile([P, V], F32, name="neg_p", tag="after_ln")
-        for b in range(BANKS):
-            nc.scalar.activation(out=neg_p[:, bank_cols(b)], in_=p_sb[:, bank_cols(b)], func=ACT.Copy, scale=neg_share[:, b : b + 1])
-        e1_sum = sb.tile([P, 1], F32, name="e1_sum", tag="after_hda")
+        e1_sum = col("e1_sum")
         nc.scalar.activation(out=e1_sum[:], in_=n1_sum[:], func=ACT.Identity, bias=sw_sum[:])
-        root_coef = col("root_coef")
-        nc.scalar.activation(out=root_coef[:], in_=e1_sum[:], func=ACT.Copy, scale=1.0 / math.sqrt(GAIN))
-        neg_e = col("neg_e")
+        hda_coef = sb.tile([P, BANKS], F32, name="hda_coef", tag="after_hda")
+        nc.scalar.activation(out=hda_coef[:], in_=neg_share[:], func=ACT.Copy, scale=e1_sum[:])
+        root_last = sb.tile([P, 1], F32, name="root_last", tag="after_last_quad")
+        nc.scalar.activation(out=root_last[:], in_=hda_coef[:, BANKS - 1 : BANKS], func=ACT.Copy, scale=1.0 / math.sqrt(GAIN))
+        root_coef = col("root_coef", BANKS - 1)
+        nc.scalar.activation(out=root_coef[:], in_=hda_coef[:, 0 : BANKS - 1], func=ACT.Copy, scale=1.0 / math.sqrt(GAIN))
+        neg_e = sb.tile([P, 1], F32, name="neg_e", tag="after_cross")
         nc.scalar.activation(out=neg_e[:], in_=e1_sum[:], func=ACT.Copy, scale=-1.0 / GAIN)
 
-        e1 = listed("e1")
-        nc.vector.tensor_tensor(out=e1[:], in0=n1[:], in1=sw_gain[:], op=ALU.add)
-        ue = listed("ue")
-        ue_sum = col("ue_sum")
-        nc.vector.scalar_tensor_tensor(out=ue[:], in0=px[:], scalar=inv_z[:], in1=e1[:], op0=ALU.mult, op1=ALU.mult, accum_out=ue_sum[:])
+        un = listed("un")
+        un_sum = col("un_sum")
+        nc.vector.scalar_tensor_tensor(out=un[:], in0=px[:], scalar=inv_z[:], in1=n1[:], op0=ALU.mult, op1=ALU.mult, accum_out=un_sum[:])
 
         hda = sb.tile([P, V], F32, name="hda")
-        nc.vector.scalar_tensor_tensor(out=hda[:], in0=neg_p[:], scalar=e1_sum[:], in1=placed[:], op0=ALU.mult, op1=ALU.add)
+        for b in range(BANKS):
+            nc.vector.scalar_tensor_tensor(
+                out=hda[:, bank_cols(b)], in0=p_sb[:, bank_cols(b)], scalar=hda_coef[:, b : b + 1],
+                in1=placed[:, bank_cols(b)], op0=ALU.mult, op1=ALU.add,
+            )
         f = sb.tile([P, I], F32, name="f", tag="after_hda")
-        nc.vector.tensor_tensor(out=f[:], in0=n1[:], in1=w[:], op=ALU.subtract)
+        nc.vector.scalar_tensor_tensor(out=f[:], in0=w[:], scalar=neg_mul[:, 0:1], in1=n1[:], op0=ALU.mult, op1=ALU.add)
         he = listed("he")
         nc.vector.tensor_scalar(out=he[:], in0=hda[:].indirect(offsets[:]), scalar1=1.0 / GAIN, scalar2=0.0, op0=ALU.mult, op1=ALU.add)
 
@@ -199,46 +208,91 @@ def tile_attend_gpfocal_heads_kernel(tc, hid, voc_words, voc_scales, mult, sw, b
             for j in range(BLOCKS):
                 nc.tensor.matmul(turned[b][:, block_cols(j)], term[:, block_cols(j)], ident[:], start=False, stop=(last and j == BLOCKS - 1), is_transpose=True)
 
+        def sum_turned(first, second, name, tag):
+            total = ps.tile([P, I], F32, name=name, tag=tag)
+            for j in range(BLOCKS):
+                nc.tensor.matmul(total[:, block_cols(j)], first[:, block_cols(j)], ident[:], start=True, stop=False, is_transpose=True)
+                nc.tensor.matmul(total[:, block_cols(j)], second[:, block_cols(j)], ident[:], start=False, stop=True, is_transpose=True)
+            return total
+
+        def turn_back(total, name, tag):
+            staged = sb.tile([P, BANK], F32, name=name + "_staged", tag=name + "_staged")
+            nc.scalar.copy(out=staged[:], in_=total[:])
+            back = ps.tile([P, BANK], F32, name=name, tag=tag)
+            for j in range(BLOCKS):
+                nc.tensor.transpose(back[:, block_cols(j)], staged[:, block_cols(j)], ident[:])
+            return back
+
+        last = BANKS - 1
+
+        def add_quadratic(b):
+            quad = sb.tile([P, BANK], F32, name="quad%d" % b)
+            nc.scalar.activation(out=quad[:], in_=p_sb[:, bank_cols(b)], func=ACT.Square, scale=root_last[:] if b == last else root_coef[:, b : b + 1])
+            add_turned(b, quad, b == last)
+
+        add_quadratic(last)
+        dense_last = turn_back(turned[last], "dense_last", "row3")
+        sq_part = col("sq_part", BANKS)
+        unused_sq = [
+            sb.tile([P, BANK], BF16, name="unused_sq", tag="after_ln"),
+            sb.tile([P, BANK], BF16, name="unused_sq_late", tag="after_last_quad"),
+        ]
+        for b in range(BANKS):
+            nc.scalar.activation(
+                out=unused_sq[b // 2][:], in_=p_sb[:, bank_cols(b)], func=ACT.Square,
+                scale=neg_share[:, b : b + 1], accum_out=sq_part[:, b : b + 1],
+            )
         sq_sum = col("sq_sum")
-        unused_sq = sb.tile([P, V], BF16, name="unused_sq")
-        nc.scalar.activation(out=unused_sq[:], in_=neg_p[:], func=ACT.Square, scale=math.sqrt(GAIN), accum_out=sq_sum[:])
+        sq_terms = col("sq_terms", BANKS)
+        nc.scalar.activation(out=sq_terms[:], in_=sq_part[:], func=ACT.Identity, scale=GAIN, accum_out=sq_sum[:])
+        for b in range(last):
+            add_quadratic(b)
+
+        g_first = col("g_first")
+        nc.scalar.activation(out=g_first[:], in_=sq_sum[:], func=ACT.Identity, scale=neg_e[:], bias=w_sum[:])
         g = col("g")
-        nc.scalar.activation(out=g[:], in_=sq_sum[:], func=ACT.Identity, scale=neg_e[:], bias=ue_sum[:])
-        centre = col("centre")
-        nc.scalar.activation(out=centre[:], in_=g[:], func=ACT.Copy, scale=-0.5 / math.sqrt(GAIN))
+        nc.scalar.activation(out=g[:], in_=un_sum[:], func=ACT.Identity, bias=g_first[:])
         g_small = col("g_small")
         nc.scalar.activation(out=g_small[:], in_=g[:], func=ACT.Copy, scale=1.0 / GAIN)
-        for b in range(BANKS):
-            quad = sb.tile([P, BANK], F32, name="quad%d" % b)
-            nc.scalar.activation(out=quad[:], in_=neg_p[:, bank_cols(b)], func=ACT.Square, scale=root_coef[:], bias=centre[:])
-            add_turned(b, quad, False)
-        centre_sq = col("centre_sq")
-        nc.scalar.activation(out=centre_sq[:], in_=centre[:], func=ACT.Square)
+        neg_ge = col("neg_ge")
+        nc.scalar.activation(out=neg_ge[:], in_=g[:], func=ACT.Copy, scale=neg_e[:])
+        ue = turn_back(sum_turned(w, un, "ue_turned", "turned3"), "ue", "row0")
         cross = listed("cross")
         nc.scalar.activation(out=cross[:], in_=ue[:], func=ACT.Copy, scale=neg_e[:])
 
-        e51 = listed("e51")
+        e51 = sb.tile([P, I], F32, name="e51", tag="e51")
         e51_sum = col("e51_sum")
         nc.vector.scalar_tensor_tensor(out=e51[:], in0=he[:], scalar=g_small[:], in1=f[:], op0=ALU.subtract, op1=ALU.mult, accum_out=e51_sum[:])
         nc.vector.tensor_tensor(out=placed[:].indirect(offsets[:]), in0=e51[:], in1=cross[:], op=ALU.add)
 
+        neg_h = sb.tile([P, 1], F32, name="neg_h", tag="after_cross")
+        nc.scalar.activation(out=neg_h[:], in_=e51_sum[:], func=ACT.Identity, bias=neg_ge[:])
+        lin_coef = col("lin_coef", BANKS)
+        nc.scalar.activation(out=lin_coef[:], in_=neg_share[:], func=ACT.Copy, scale=neg_h[:])
+
         def add_linear(b):
             lin = sb.tile([P, BANK], F32, name="lin%d" % b)
-            nc.scalar.activation(out=lin[:], in_=neg_p[:, bank_cols(b)], func=ACT.Copy, scale=e51_sum[:])
+            nc.scalar.activation(out=lin[:], in_=p_sb[:, bank_cols(b)], func=ACT.Copy, scale=lin_coef[:, b : b + 1])
             add_turned(b, lin, True)
 
-        def finish(b):
-            dense_t = sb.tile([P, BANK], F32, name="dense_t%d" % b)
-            nc.scalar.copy(out=dense_t[:], in_=turned[b][:])
-            dense = ps.tile([P, BANK], F32, name="dense", tag="row%d" % b)
-            for j in range(BLOCKS):
-                nc.tensor.transpose(dense[:, block_cols(j)], dense_t[:, block_cols(j)], ident[:])
-            res = sb.tile([P, BANK], F32, name="res%d" % b)
-            nc.vector.scalar_tensor_tensor(out=res[:], in0=dense[:], scalar=centre_sq[:], in1=placed[:, bank_cols(b)], op0=ALU.subtract, op1=ALU.add)
-            nc.sync.dma_start(out=out[:, bank_cols(b)], in_=res[:])
+        def store(b, dense, cols):
+            res = sb.tile([P, cols.stop - cols.start], F32, name="res%d" % cols.start)
+            first = b * BANK
+            nc.vector.tensor_tensor(out=res[:], in0=dense[:, cols.start - first : cols.stop - first], in1=placed[:, cols], op=ALU.add)
+            nc.sync.dma_start(out=out[:, cols], in_=res[:])
 
-        add_linear(0)
-        for b in range(BANKS):
-            if b + 1 < BANKS:
-                add_linear(b + 1)
-            finish(b)
+        with_lin = sb.tile([P, BANK], F32, name="with_lin")
+        nc.vector.scalar_tensor_tensor(
+            out=with_lin[:], in0=p_sb[:, bank_cols(last)], scalar=lin_coef[:, last : last + 1], in1=dense_last[:], op0=ALU.mult, op1=ALU.add
+        )
+        store(last, with_lin, bank_cols(last))
+
+        for b in range(last):
+            add_linear(b)
+        for b in range(last):
+            dense = turn_back(turned[b], "dense%d" % b, "row%d" % b)
+            if b + 1 < last:
+                store(b, dense, bank_cols(b))
+            else:
+                store(b, dense, slice(b * BANK, (b + 1) * BANK - P))
+                store(b, dense, slice((b + 1) * BANK - P, (b + 1) * BANK))

@@ -47,8 +47,6 @@ def tile_attend_gpfocal_heads_kernel(tc, hid, voc_words, voc_scales, mult, sw, b
         def block_cols(j):
             return slice(j * P, (j + 1) * P)
 
-        sw_cols = sb.tile([P, PACK], F32, name="sw_cols", tag="sw_first", align_bytes=64)
-        nc.sync.dma_start(out=sw_cols[:], in_=sw.rearrange("o (p c) -> p (o c)", c=PACK))
         hid_raw = sb.tile([P, PACK, Q], F32, name="hid_raw")
         nc.sync.dma_start(out=hid_raw[:], in_=hid.rearrange("(p t) q -> p t q", t=PACK))
         voc_sc = sb.tile([P, V], U8, name="voc_sc", align_bytes=64)
@@ -58,12 +56,16 @@ def tile_attend_gpfocal_heads_kernel(tc, hid, voc_words, voc_scales, mult, sw, b
                 in_=voc_scales[0, g:16:4, :].bitcast(I32),
             )
         voc_w = []
-        for h in range(2):
-            t = sb.tile([P, V], U8, name="voc_w%d" % h, align_bytes=64)
-            nc.sync.dma_start(out=t[:].bitcast(I32), in_=voc_words[0, :, h * V : (h + 1) * V].bitcast(I32))
-            voc_w.append(t)
+        for first, count in ((0, 1), (1, 1), (2, 2)):
+            t = sb.tile([P, count * 2 * BANK], U8, name="voc_w%d" % first, align_bytes=64)
+            nc.sync.dma_start(
+                out=t[:].bitcast(I32), in_=voc_words[0, :, first * 2 * BANK : (first + count) * 2 * BANK].bitcast(I32)
+            )
+            voc_w.extend(t[:, k * 2 * BANK : (k + 1) * 2 * BANK] for k in range(count))
         offsets = sb.tile([P, I // 16], U16, name="offsets")
         nc.sync.dma_start(offsets[:], offs)
+        sw_cols = col("sw_cols", PACK)
+        nc.sync.dma_start(out=sw_cols[:], in_=sw.rearrange("o (p c) -> p (o c)", c=PACK))
         mul_col = col("mul_col")
         nc.sync.dma_start(out=mul_col[:], in_=mult)
 
@@ -72,23 +74,10 @@ def tile_attend_gpfocal_heads_kernel(tc, hid, voc_words, voc_scales, mult, sw, b
         ident = sb.tile([P, P], F32, name="ident")
         make_identity(nc, ident[:])
 
-        sw_ps = ps.tile([P, BANK], F32, name="sw_ps", tag="turned3")
-        for c in range(PACK):
-            nc.tensor.transpose(sw_ps[:, block_cols(c)], sw_cols[:, c : c + 1].to_broadcast([P, P]), ident[:])
-        sw_gain = listed("sw_gain")
-        sw_sum = col("sw_sum")
-        nc.scalar.activation(
-            out=sw_gain[:].rearrange("q (p c) -> q p c", c=PACK),
-            in_=sw_ps[:].rearrange("q (c p) -> q p c", c=PACK),
-            func=ACT.Identity,
-            scale=GAIN,
-            accum_out=sw_sum[:],
-        )
-
         hid_bf = sb.tile([P, Q, PACK], BF16, name="hid_bf", tag="hold", align_bytes=64)
         nc.vector.tensor_copy(out=hid_bf[:], in_=hid_raw[:].rearrange("p t q -> p q t"))
         hid_codes = sb.tile([P, Q], U32, name="hid_codes", align_bytes=64)
-        hid_sc = sb.tile([P, Q], U8, name="hid_sc", tag="sw_first", align_bytes=64)
+        hid_sc = sb.tile([P, Q], U8, name="hid_sc", align_bytes=64)
         nc.vector.quantize_mx(
             out=hid_codes[:].bitcast(FP8X4), scales=hid_sc[:], in_=hid_bf[:].rearrange("p q t -> p (q t)")
         )
@@ -101,12 +90,11 @@ def tile_attend_gpfocal_heads_kernel(tc, hid, voc_words, voc_scales, mult, sw, b
         z_part = col("z_part", BANKS)
         for b in range(BANKS):
             a_ps = ps.tile([P, BANK], F32, name="a_ps", tag="row%d" % b)
-            half, part = divmod(b, 2)
             nc.tensor.matmul_mx(
                 out=a_ps[:],
                 lhsT=hid_codes[:].bitcast(FP8X4),
                 lhsT_scale=hid_sc[:],
-                rhs=voc_w[half][:, part * 2 * BANK : (part + 1) * 2 * BANK].bitcast(FP4X4),
+                rhs=voc_w[b].bitcast(FP4X4),
                 rhs_scale=voc_sc[:, bank_cols(b)],
                 start=True,
                 stop=True,
@@ -119,6 +107,19 @@ def tile_attend_gpfocal_heads_kernel(tc, hid, voc_words, voc_scales, mult, sw, b
                 out=p_sb[:, bank_cols(b)], in_=neg_a[:, bank_cols(b)], func=ACT.Exp, scale=-1.0,
                 bias=neg_max[:, b : b + 1], accum_out=z_part[:, b : b + 1],
             )
+        sw_ps = ps.tile([P, BANK], F32, name="sw_ps", tag="row3")
+        for c in range(PACK):
+            nc.tensor.transpose(sw_ps[:, block_cols(c)], sw_cols[:, c : c + 1].to_broadcast([P, P]), ident[:])
+        sw_gain = listed("sw_gain")
+        sw_sum = col("sw_sum")
+        nc.scalar.activation(
+            out=sw_gain[:].rearrange("q (p c) -> q p c", c=PACK),
+            in_=sw_ps[:].rearrange("q (c p) -> q p c", c=PACK),
+            func=ACT.Identity,
+            scale=GAIN,
+            accum_out=sw_sum[:],
+        )
+
         neg_m1 = col("neg_m1")
         nc.vector.tensor_reduce(out=neg_m1[:], in_=neg_max[:], axis=mybir.AxisListType.X, op=ALU.min)
         neg_ax = listed("neg_ax")
@@ -175,10 +176,8 @@ def tile_attend_gpfocal_heads_kernel(tc, hid, voc_words, voc_scales, mult, sw, b
         nc.scalar.activation(out=e1_sum[:], in_=n1_sum[:], func=ACT.Identity, bias=sw_sum[:])
         hda_coef = sb.tile([P, BANKS], F32, name="hda_coef", tag="after_hda")
         nc.scalar.activation(out=hda_coef[:], in_=neg_share[:], func=ACT.Copy, scale=e1_sum[:])
-        root_last = sb.tile([P, 1], F32, name="root_last", tag="after_last_quad")
-        nc.scalar.activation(out=root_last[:], in_=hda_coef[:, BANKS - 1 : BANKS], func=ACT.Copy, scale=1.0 / math.sqrt(GAIN))
-        root_coef = col("root_coef", BANKS - 1)
-        nc.scalar.activation(out=root_coef[:], in_=hda_coef[:, 0 : BANKS - 1], func=ACT.Copy, scale=1.0 / math.sqrt(GAIN))
+        root_coef = sb.tile([P, BANKS], F32, name="root_coef", tag="after_quads")
+        nc.scalar.activation(out=root_coef[:], in_=hda_coef[:], func=ACT.Copy, scale=1.0 / math.sqrt(GAIN))
         neg_e = sb.tile([P, 1], F32, name="neg_e", tag="after_cross")
         nc.scalar.activation(out=neg_e[:], in_=e1_sum[:], func=ACT.Copy, scale=-1.0 / GAIN)
 
@@ -227,15 +226,17 @@ def tile_attend_gpfocal_heads_kernel(tc, hid, voc_words, voc_scales, mult, sw, b
 
         def add_quadratic(b):
             quad = sb.tile([P, BANK], F32, name="quad%d" % b)
-            nc.scalar.activation(out=quad[:], in_=p_sb[:, bank_cols(b)], func=ACT.Square, scale=root_last[:] if b == last else root_coef[:, b : b + 1])
+            nc.scalar.activation(out=quad[:], in_=p_sb[:, bank_cols(b)], func=ACT.Square, scale=root_coef[:, b : b + 1])
             add_turned(b, quad, b == last)
 
         add_quadratic(last)
         dense_last = turn_back(turned[last], "dense_last", "row3")
+        for b in range(last):
+            add_quadratic(b)
         sq_part = col("sq_part", BANKS)
         unused_sq = [
             sb.tile([P, BANK], BF16, name="unused_sq", tag="after_ln"),
-            sb.tile([P, BANK], BF16, name="unused_sq_late", tag="after_last_quad"),
+            sb.tile([P, BANK], BF16, name="unused_sq_late", tag="after_quads"),
         ]
         for b in range(BANKS):
             nc.scalar.activation(
@@ -245,8 +246,6 @@ def tile_attend_gpfocal_heads_kernel(tc, hid, voc_words, voc_scales, mult, sw, b
         sq_sum = col("sq_sum")
         sq_terms = col("sq_terms", BANKS)
         nc.scalar.activation(out=sq_terms[:], in_=sq_part[:], func=ACT.Identity, scale=GAIN, accum_out=sq_sum[:])
-        for b in range(last):
-            add_quadratic(b)
 
         g_first = col("g_first")
         nc.scalar.activation(out=g_first[:], in_=sq_sum[:], func=ACT.Identity, scale=neg_e[:], bias=w_sum[:])
@@ -285,7 +284,8 @@ def tile_attend_gpfocal_heads_kernel(tc, hid, voc_words, voc_scales, mult, sw, b
         nc.vector.scalar_tensor_tensor(
             out=with_lin[:], in0=p_sb[:, bank_cols(last)], scalar=lin_coef[:, last : last + 1], in1=dense_last[:], op0=ALU.mult, op1=ALU.add
         )
-        store(last, with_lin, bank_cols(last))
+        store(last, with_lin, slice(last * BANK, last * BANK + P))
+        store(last, with_lin, slice(last * BANK + P, V))
 
         for b in range(last):
             add_linear(b)

@@ -20,12 +20,16 @@ ACT = mybir.ActivationFunctionType
 
 P = 128
 PACK = 4
+QUADRANT = 32
+SCALE_ROWS = D // 32
+WORD_BYTES = 2
 BANK = 512
 BANKS = V // BANK
+LAST = BANKS - 1
 BLOCKS = BANK // P
 GAIN = 64.0 * 2.0 * 64.0
-LN2 = math.log(2.0)
-GUESS_SLOPE = -LN2 / 2.0**23
+WORD_LOADS = ((0, 1), (1, 1), (2, 2))
+GUESS_SLOPE = -math.log(2.0) / 2.0**23
 GUESS_OFFSET = 88.0
 
 
@@ -50,22 +54,24 @@ def tile_attend_gpfocal_heads_kernel(tc, hid, voc_words, voc_scales, mult, sw, b
         hid_raw = sb.tile([P, PACK, Q], F32, name="hid_raw")
         nc.sync.dma_start(out=hid_raw[:], in_=hid.rearrange("(p t) q -> p t q", t=PACK))
         voc_sc = sb.tile([P, V], U8, name="voc_sc", align_bytes=64)
-        for g in range(4):
+        for r in range(PACK):
             nc.sync.dma_start(
-                out=voc_sc[g:P:32, :].bitcast(I32),
-                in_=voc_scales[0, g:16:4, :].bitcast(I32),
+                out=voc_sc[r:P:QUADRANT, :].bitcast(I32),
+                in_=voc_scales[0, r:SCALE_ROWS:PACK, :].bitcast(I32),
             )
+        bank_bytes = WORD_BYTES * BANK
         voc_w = []
-        for first, count in ((0, 1), (1, 1), (2, 2)):
-            t = sb.tile([P, count * 2 * BANK], U8, name="voc_w%d" % first, align_bytes=64)
+        for first, count in WORD_LOADS:
+            words = sb.tile([P, count * bank_bytes], U8, name="voc_w%d" % first, align_bytes=64)
             nc.sync.dma_start(
-                out=t[:].bitcast(I32), in_=voc_words[0, :, first * 2 * BANK : (first + count) * 2 * BANK].bitcast(I32)
+                out=words[:].bitcast(I32),
+                in_=voc_words[0, :, first * bank_bytes : (first + count) * bank_bytes].bitcast(I32),
             )
-            voc_w.extend(t[:, k * 2 * BANK : (k + 1) * 2 * BANK] for k in range(count))
+            voc_w.extend(words[:, k * bank_bytes : (k + 1) * bank_bytes] for k in range(count))
         offsets = sb.tile([P, I // 16], U16, name="offsets")
         nc.sync.dma_start(offsets[:], offs)
-        sw_cols = col("sw_cols", PACK)
-        nc.sync.dma_start(out=sw_cols[:], in_=sw.rearrange("o (p c) -> p (o c)", c=PACK))
+        sw_cols = col("sw_cols", BLOCKS)
+        nc.sync.dma_start(out=sw_cols[:], in_=sw.rearrange("o (p c) -> p (o c)", c=BLOCKS))
         mul_col = col("mul_col")
         nc.sync.dma_start(out=mul_col[:], in_=mult)
 
@@ -74,19 +80,19 @@ def tile_attend_gpfocal_heads_kernel(tc, hid, voc_words, voc_scales, mult, sw, b
         ident = sb.tile([P, P], F32, name="ident")
         make_identity(nc, ident[:])
 
-        hid_bf = sb.tile([P, Q, PACK], BF16, name="hid_bf", tag="hold", align_bytes=64)
+        hid_bf = sb.tile([P, Q, PACK], BF16, name="hid_bf", tag="after_quantise", align_bytes=64)
         nc.vector.tensor_copy(out=hid_bf[:], in_=hid_raw[:].rearrange("p t q -> p q t"))
         hid_codes = sb.tile([P, Q], U32, name="hid_codes", align_bytes=64)
         hid_sc = sb.tile([P, Q], U8, name="hid_sc", align_bytes=64)
         nc.vector.quantize_mx(
             out=hid_codes[:].bitcast(FP8X4), scales=hid_sc[:], in_=hid_bf[:].rearrange("p q t -> p (q t)")
         )
-        base_sb = sb.tile([P, V], F32, name="base_sb", tag="hold", align_bytes=64)
+        base_sb = sb.tile([P, V], F32, name="base_sb", tag="after_quantise", align_bytes=64)
         nc.sync.dma_start(out=base_sb[:], in_=base)
 
         neg_a = sb.tile([P, V], F32, name="neg_a")
-        p_sb = sb.tile([P, V], F32, name="p_sb")
-        neg_max = sb.tile([P, BANKS], F32, name="neg_max", tag="after_max")
+        p_bank = sb.tile([P, V], F32, name="p_bank")
+        neg_max = sb.tile([P, BANKS], F32, name="neg_max", tag="after_rescale")
         z_part = col("z_part", BANKS)
         for b in range(BANKS):
             a_ps = ps.tile([P, BANK], F32, name="a_ps", tag="row%d" % b)
@@ -104,17 +110,18 @@ def tile_attend_gpfocal_heads_kernel(tc, hid, voc_words, voc_scales, mult, sw, b
                 op0=ALU.mult, op1=ALU.min, accum_out=neg_max[:, b : b + 1],
             )
             nc.scalar.activation(
-                out=p_sb[:, bank_cols(b)], in_=neg_a[:, bank_cols(b)], func=ACT.Exp, scale=-1.0,
+                out=p_bank[:, bank_cols(b)], in_=neg_a[:, bank_cols(b)], func=ACT.Exp, scale=-1.0,
                 bias=neg_max[:, b : b + 1], accum_out=z_part[:, b : b + 1],
             )
-        sw_ps = ps.tile([P, BANK], F32, name="sw_ps", tag="row3")
-        for c in range(PACK):
+
+        sw_ps = ps.tile([P, BANK], F32, name="sw_ps", tag="row%d" % LAST)
+        for c in range(BLOCKS):
             nc.tensor.transpose(sw_ps[:, block_cols(c)], sw_cols[:, c : c + 1].to_broadcast([P, P]), ident[:])
         sw_gain = listed("sw_gain")
         sw_sum = col("sw_sum")
         nc.scalar.activation(
-            out=sw_gain[:].rearrange("q (p c) -> q p c", c=PACK),
-            in_=sw_ps[:].rearrange("q (c p) -> q p c", c=PACK),
+            out=sw_gain[:].rearrange("q (p c) -> q p c", c=BLOCKS),
+            in_=sw_ps[:].rearrange("q (c p) -> q p c", c=BLOCKS),
             func=ACT.Identity,
             scale=GAIN,
             accum_out=sw_sum[:],
@@ -135,164 +142,208 @@ def tile_attend_gpfocal_heads_kernel(tc, hid, voc_words, voc_scales, mult, sw, b
         nc.vector.scalar_tensor_tensor(
             out=z_terms[:], in0=rescale[:], scalar=1.0, in1=z_part[:], op0=ALU.mult, op1=ALU.mult, accum_out=z[:]
         )
-        neg_mul = sb.tile([P, 2], F32, name="neg_mul", tag="after_max")
+        neg_mul = sb.tile([P, 2], F32, name="neg_mul", tag="after_rescale")
         nc.vector.tensor_scalar(out=neg_mul[:, 0:1], in0=mul_col[:], scalar1=-1.0, scalar2=None, op0=ALU.mult)
         nc.vector.tensor_scalar(out=neg_mul[:, 1:2], in0=mul_col[:], scalar1=-0.5, scalar2=None, op0=ALU.mult)
-        mul_ax = listed("mul_ax")
-        nc.vector.tensor_scalar(out=mul_ax[:], in0=neg_ax[:], scalar1=mul_col[:], scalar2=None, op0=ALU.mult)
+        neg_mul_ax = listed("neg_mul_ax")
+        nc.vector.tensor_scalar(out=neg_mul_ax[:], in0=neg_ax[:], scalar1=mul_col[:], scalar2=None, op0=ALU.mult)
         inv_z = col("inv_z")
         nc.vector.reciprocal(out=inv_z[:], in_=z[:])
-        neg_y0h = col("neg_y0h")
-        nc.vector.tensor_scalar(out=neg_y0h[:], in0=z[:].bitcast(I32), scalar1=GUESS_SLOPE, scalar2=GUESS_OFFSET - 0.5, op0=ALU.mult, op1=ALU.add)
-        neg_y0k = col("neg_y0k")
-        nc.vector.tensor_scalar(out=neg_y0k[:], in0=z[:].bitcast(I32), scalar1=GUESS_SLOPE, scalar2=GUESS_OFFSET + 1.5, op0=ALU.mult, op1=ALU.add)
+
+        neg_y0_exp = col("neg_y0_exp")
+        nc.vector.tensor_scalar(
+            out=neg_y0_exp[:], in0=z[:].bitcast(I32), scalar1=GUESS_SLOPE, scalar2=GUESS_OFFSET - 0.5,
+            op0=ALU.mult, op1=ALU.add,
+        )
+        neg_y0_shift = col("neg_y0_shift")
+        nc.vector.tensor_scalar(
+            out=neg_y0_shift[:], in0=z[:].bitcast(I32), scalar1=GUESS_SLOPE, scalar2=GUESS_OFFSET + 1.5,
+            op0=ALU.mult, op1=ALU.add,
+        )
         mul_z = col("mul_z")
         nc.vector.tensor_tensor(out=mul_z[:], in0=z[:], in1=mul_col[:], op=ALU.mult)
-        neg_k0 = col("neg_k0")
-        nc.vector.tensor_scalar(out=neg_k0[:], in0=neg_y0k[:], scalar1=neg_m1[:], scalar2=neg_mul[:, 0:1], op0=ALU.add, op1=ALU.mult)
-        neg_share = col("neg_share", BANKS)
-        nc.vector.tensor_scalar(out=neg_share[:], in0=rescale[:], scalar1=inv_z[:], scalar2=-1.0, op0=ALU.mult, op1=ALU.mult)
+        shift0 = col("shift0")
+        nc.vector.tensor_scalar(
+            out=shift0[:], in0=neg_y0_shift[:], scalar1=neg_m1[:], scalar2=neg_mul[:, 0:1], op0=ALU.add, op1=ALU.mult
+        )
+        to_neg_share = col("to_neg_share", BANKS)
+        nc.vector.tensor_scalar(
+            out=to_neg_share[:], in0=rescale[:], scalar1=inv_z[:], scalar2=-1.0, op0=ALU.mult, op1=ALU.mult
+        )
 
-        ex0 = col("ex0")
-        sq0 = col("sq0")
-        ex1 = sb.tile([P, 1], F32, name="ex1", tag="after_ln")
-        neg_k1 = col("neg_k1")
-        neg_shift = col("neg_shift")
-        nc.scalar.activation(out=ex0[:], in_=z[:].bitcast(U32), func=ACT.Exp, scale=GUESS_SLOPE, bias=GUESS_OFFSET)
-        nc.scalar.activation(out=sq0[:], in_=ex0[:], func=ACT.Square, scale=z[:], bias=-2.0)
-        nc.scalar.activation(out=ex1[:], in_=sq0[:], func=ACT.Exp, scale=0.5, bias=neg_y0h[:])
-        nc.scalar.activation(out=neg_k1[:], in_=sq0[:], func=ACT.Identity, scale=neg_mul[:, 1:2], bias=neg_k0[:])
-        nc.scalar.activation(out=neg_shift[:], in_=ex1[:], func=ACT.Identity, scale=mul_z[:], bias=neg_k1[:])
+        exp0 = col("exp0")
+        square0 = col("square0")
+        exp1 = sb.tile([P, 1], F32, name="exp1", tag="after_ln")
+        shift1 = col("shift1")
+        shift = col("shift")
+        nc.scalar.activation(out=exp0[:], in_=z[:].bitcast(U32), func=ACT.Exp, scale=GUESS_SLOPE, bias=GUESS_OFFSET)
+        nc.scalar.activation(out=square0[:], in_=exp0[:], func=ACT.Square, scale=z[:], bias=-2.0)
+        nc.scalar.activation(out=exp1[:], in_=square0[:], func=ACT.Exp, scale=0.5, bias=neg_y0_exp[:])
+        nc.scalar.activation(out=shift1[:], in_=square0[:], func=ACT.Identity, scale=neg_mul[:, 1:2], bias=shift0[:])
+        nc.scalar.activation(out=shift[:], in_=exp1[:], func=ACT.Identity, scale=mul_z[:], bias=shift1[:])
 
-        w = listed("w")
-        w_sum = col("w_sum")
-        nc.vector.scalar_tensor_tensor(out=w[:], in0=px[:], scalar=inv_z[:], in1=sw_gain[:], op0=ALU.mult, op1=ALU.mult, accum_out=w_sum[:])
-        n1 = listed("n1")
-        n1_sum = col("n1_sum")
-        nc.vector.scalar_tensor_tensor(out=n1[:], in0=mul_ax[:], scalar=neg_shift[:], in1=w[:], op0=ALU.add, op1=ALU.mult, accum_out=n1_sum[:])
-        nc.vector.tensor_tensor(out=placed[:].indirect(offsets[:]), in0=n1[:], in1=sw_gain[:], op=ALU.add)
+        us = listed("us")
+        us_sum = col("us_sum")
+        nc.vector.scalar_tensor_tensor(
+            out=us[:], in0=px[:], scalar=inv_z[:], in1=sw_gain[:], op0=ALU.mult, op1=ALU.mult, accum_out=us_sum[:]
+        )
+        focal = listed("focal")
+        focal_sum = col("focal_sum")
+        nc.vector.scalar_tensor_tensor(
+            out=focal[:], in0=neg_mul_ax[:], scalar=shift[:], in1=us[:], op0=ALU.add, op1=ALU.mult,
+            accum_out=focal_sum[:],
+        )
+        nc.vector.tensor_tensor(out=placed[:].indirect(offsets[:]), in0=focal[:], in1=sw_gain[:], op=ALU.add)
 
-        e1_sum = col("e1_sum")
-        nc.scalar.activation(out=e1_sum[:], in_=n1_sum[:], func=ACT.Identity, bias=sw_sum[:])
-        hda_coef = sb.tile([P, BANKS], F32, name="hda_coef", tag="after_hda")
-        nc.scalar.activation(out=hda_coef[:], in_=neg_share[:], func=ACT.Copy, scale=e1_sum[:])
+        gain_e = col("gain_e")
+        nc.scalar.activation(out=gain_e[:], in_=focal_sum[:], func=ACT.Identity, bias=sw_sum[:])
+        hda_coef = sb.tile([P, LAST], F32, name="hda_coef", tag="after_hda")
+        nc.scalar.activation(out=hda_coef[:], in_=to_neg_share[:, 0:LAST], func=ACT.Copy, scale=gain_e[:])
+        hda_coef_last = col("hda_coef_last")
+        nc.scalar.activation(out=hda_coef_last[:], in_=to_neg_share[:, LAST:BANKS], func=ACT.Copy, scale=gain_e[:])
+        root_e = col("root_e")
+        nc.scalar.activation(out=root_e[:], in_=gain_e[:], func=ACT.Copy, scale=1.0 / math.sqrt(GAIN))
         root_coef = sb.tile([P, BANKS], F32, name="root_coef", tag="after_quads")
-        nc.scalar.activation(out=root_coef[:], in_=hda_coef[:], func=ACT.Copy, scale=1.0 / math.sqrt(GAIN))
+        nc.scalar.activation(out=root_coef[:], in_=to_neg_share[:], func=ACT.Copy, scale=root_e[:])
         neg_e = sb.tile([P, 1], F32, name="neg_e", tag="after_cross")
-        nc.scalar.activation(out=neg_e[:], in_=e1_sum[:], func=ACT.Copy, scale=-1.0 / GAIN)
+        nc.scalar.activation(out=neg_e[:], in_=gain_e[:], func=ACT.Copy, scale=-1.0 / GAIN)
 
-        un = listed("un")
-        un_sum = col("un_sum")
-        nc.vector.scalar_tensor_tensor(out=un[:], in0=px[:], scalar=inv_z[:], in1=n1[:], op0=ALU.mult, op1=ALU.mult, accum_out=un_sum[:])
+        u_focal = listed("u_focal")
+        u_focal_sum = col("u_focal_sum")
+        nc.vector.scalar_tensor_tensor(
+            out=u_focal[:], in0=px[:], scalar=inv_z[:], in1=focal[:], op0=ALU.mult, op1=ALU.mult,
+            accum_out=u_focal_sum[:],
+        )
 
         hda = sb.tile([P, V], F32, name="hda")
         for b in range(BANKS):
             nc.vector.scalar_tensor_tensor(
-                out=hda[:, bank_cols(b)], in0=p_sb[:, bank_cols(b)], scalar=hda_coef[:, b : b + 1],
+                out=hda[:, bank_cols(b)], in0=p_bank[:, bank_cols(b)], scalar=hda_coef[:, b : b + 1] if b < LAST else hda_coef_last[:],
                 in1=placed[:, bank_cols(b)], op0=ALU.mult, op1=ALU.add,
             )
-        f = sb.tile([P, I], F32, name="f", tag="after_hda")
-        nc.vector.scalar_tensor_tensor(out=f[:], in0=w[:], scalar=neg_mul[:, 0:1], in1=n1[:], op0=ALU.mult, op1=ALU.add)
-        he = listed("he")
-        nc.vector.tensor_scalar(out=he[:], in0=hda[:].indirect(offsets[:]), scalar1=1.0 / GAIN, scalar2=0.0, op0=ALU.mult, op1=ALU.add)
+        gain_f = sb.tile([P, I], F32, name="gain_f", tag="after_hda")
+        nc.vector.scalar_tensor_tensor(
+            out=gain_f[:], in0=us[:], scalar=neg_mul[:, 0:1], in1=focal[:], op0=ALU.mult, op1=ALU.add
+        )
+        he_over_gain = listed("he_over_gain")
+        nc.vector.tensor_scalar(
+            out=he_over_gain[:], in0=hda[:].indirect(offsets[:]), scalar1=1.0 / GAIN, scalar2=0.0,
+            op0=ALU.mult, op1=ALU.add,
+        )
 
         turned = []
         for b in range(BANKS):
-            t_ps = ps.tile([P, BANK], F32, name="t_ps", tag="turned%d" % b)
-            turned.append(t_ps)
+            bank_sum = ps.tile([P, BANK], F32, name="bank_sum", tag="turned%d" % b)
+            turned.append(bank_sum)
             for j in range(BLOCKS):
-                nc.tensor.matmul(t_ps[:, block_cols(j)], base_sb[:, block_cols(b * BLOCKS + j)], ident[:], start=(j == 0), stop=False, is_transpose=True)
+                nc.tensor.matmul(
+                    bank_sum[:, block_cols(j)], base_sb[:, block_cols(b * BLOCKS + j)], ident[:],
+                    start=(j == 0), stop=False, is_transpose=True,
+                )
 
-        def add_turned(b, term, last):
+        def add_turned(b, term, closes):
             for j in range(BLOCKS):
-                nc.tensor.matmul(turned[b][:, block_cols(j)], term[:, block_cols(j)], ident[:], start=False, stop=(last and j == BLOCKS - 1), is_transpose=True)
-
-        def sum_turned(first, second, name, tag):
-            total = ps.tile([P, I], F32, name=name, tag=tag)
-            for j in range(BLOCKS):
-                nc.tensor.matmul(total[:, block_cols(j)], first[:, block_cols(j)], ident[:], start=True, stop=False, is_transpose=True)
-                nc.tensor.matmul(total[:, block_cols(j)], second[:, block_cols(j)], ident[:], start=False, stop=True, is_transpose=True)
-            return total
+                nc.tensor.matmul(
+                    turned[b][:, block_cols(j)], term[:, block_cols(j)], ident[:],
+                    start=False, stop=(closes and j == BLOCKS - 1), is_transpose=True,
+                )
 
         def turn_back(total, name, tag):
-            staged = sb.tile([P, BANK], F32, name=name + "_staged", tag=name + "_staged")
+            staged = sb.tile([P, BANK], F32, name=name + "_staged")
             nc.scalar.copy(out=staged[:], in_=total[:])
             back = ps.tile([P, BANK], F32, name=name, tag=tag)
             for j in range(BLOCKS):
                 nc.tensor.transpose(back[:, block_cols(j)], staged[:, block_cols(j)], ident[:])
             return back
 
-        last = BANKS - 1
-
         def add_quadratic(b):
             quad = sb.tile([P, BANK], F32, name="quad%d" % b)
-            nc.scalar.activation(out=quad[:], in_=p_sb[:, bank_cols(b)], func=ACT.Square, scale=root_coef[:, b : b + 1])
-            add_turned(b, quad, b == last)
+            nc.scalar.activation(
+                out=quad[:], in_=p_bank[:, bank_cols(b)], func=ACT.Square, scale=root_coef[:, b : b + 1]
+            )
+            add_turned(b, quad, b == LAST)
 
-        add_quadratic(last)
-        dense_last = turn_back(turned[last], "dense_last", "row3")
-        for b in range(last):
+        add_quadratic(LAST)
+        dense_last = turn_back(turned[LAST], "dense_last", "row%d" % LAST)
+        for b in range(LAST):
             add_quadratic(b)
+
         sq_part = col("sq_part", BANKS)
-        unused_sq = [
-            sb.tile([P, BANK], BF16, name="unused_sq", tag="after_ln"),
-            sb.tile([P, BANK], BF16, name="unused_sq_late", tag="after_quads"),
+        squares = [
+            sb.tile([P, BANK], BF16, name="squares_early", tag="after_ln"),
+            sb.tile([P, BANK], BF16, name="squares_late", tag="after_quads"),
         ]
         for b in range(BANKS):
             nc.scalar.activation(
-                out=unused_sq[b // 2][:], in_=p_sb[:, bank_cols(b)], func=ACT.Square,
-                scale=neg_share[:, b : b + 1], accum_out=sq_part[:, b : b + 1],
+                out=squares[b // 2][:], in_=p_bank[:, bank_cols(b)], func=ACT.Square,
+                scale=to_neg_share[:, b : b + 1], accum_out=sq_part[:, b : b + 1],
             )
-        sq_sum = col("sq_sum")
+        gain_sq_sum = col("gain_sq_sum")
         sq_terms = col("sq_terms", BANKS)
-        nc.scalar.activation(out=sq_terms[:], in_=sq_part[:], func=ACT.Identity, scale=GAIN, accum_out=sq_sum[:])
+        nc.scalar.activation(out=sq_terms[:], in_=sq_part[:], func=ACT.Identity, scale=GAIN, accum_out=gain_sq_sum[:])
 
-        g_first = col("g_first")
-        nc.scalar.activation(out=g_first[:], in_=sq_sum[:], func=ACT.Identity, scale=neg_e[:], bias=w_sum[:])
+        g_part = col("g_part")
+        nc.scalar.activation(out=g_part[:], in_=gain_sq_sum[:], func=ACT.Identity, scale=neg_e[:], bias=us_sum[:])
         g = col("g")
-        nc.scalar.activation(out=g[:], in_=un_sum[:], func=ACT.Identity, bias=g_first[:])
-        g_small = col("g_small")
-        nc.scalar.activation(out=g_small[:], in_=g[:], func=ACT.Copy, scale=1.0 / GAIN)
+        nc.scalar.activation(out=g[:], in_=u_focal_sum[:], func=ACT.Identity, bias=g_part[:])
+        g_over_gain = col("g_over_gain")
+        nc.scalar.activation(out=g_over_gain[:], in_=g[:], func=ACT.Copy, scale=1.0 / GAIN)
         neg_ge = col("neg_ge")
         nc.scalar.activation(out=neg_ge[:], in_=g[:], func=ACT.Copy, scale=neg_e[:])
-        ue = turn_back(sum_turned(w, un, "ue_turned", "turned3"), "ue", "row0")
+        lin_early = col("lin_early", BANKS)
+        nc.scalar.activation(out=lin_early[:], in_=to_neg_share[:], func=ACT.Copy, scale=neg_ge[:])
+
+        ue_turned = ps.tile([P, I], F32, name="ue_turned", tag="turned%d" % LAST)
+        for j in range(BLOCKS):
+            for term, opens in ((us, True), (u_focal, False)):
+                nc.tensor.matmul(
+                    ue_turned[:, block_cols(j)], term[:, block_cols(j)], ident[:],
+                    start=opens, stop=not opens, is_transpose=True,
+                )
+        ue = turn_back(ue_turned, "ue", "row0")
         cross = listed("cross")
         nc.scalar.activation(out=cross[:], in_=ue[:], func=ACT.Copy, scale=neg_e[:])
 
-        e51 = sb.tile([P, I], F32, name="e51", tag="e51")
+        e51 = listed("e51")
         e51_sum = col("e51_sum")
-        nc.vector.scalar_tensor_tensor(out=e51[:], in0=he[:], scalar=g_small[:], in1=f[:], op0=ALU.subtract, op1=ALU.mult, accum_out=e51_sum[:])
+        nc.vector.scalar_tensor_tensor(
+            out=e51[:], in0=he_over_gain[:], scalar=g_over_gain[:], in1=gain_f[:], op0=ALU.subtract, op1=ALU.mult,
+            accum_out=e51_sum[:],
+        )
         nc.vector.tensor_tensor(out=placed[:].indirect(offsets[:]), in0=e51[:], in1=cross[:], op=ALU.add)
 
-        neg_h = sb.tile([P, 1], F32, name="neg_h", tag="after_cross")
-        nc.scalar.activation(out=neg_h[:], in_=e51_sum[:], func=ACT.Identity, bias=neg_ge[:])
-        lin_coef = col("lin_coef", BANKS)
-        nc.scalar.activation(out=lin_coef[:], in_=neg_share[:], func=ACT.Copy, scale=neg_h[:])
+        lin_coef = sb.tile([P, BANKS], F32, name="lin_coef", tag="after_cross")
+        for b in range(BANKS):
+            nc.scalar.activation(
+                out=lin_coef[:, b : b + 1], in_=e51_sum[:], func=ACT.Identity,
+                scale=to_neg_share[:, b : b + 1], bias=lin_early[:, b : b + 1],
+            )
 
         def add_linear(b):
             lin = sb.tile([P, BANK], F32, name="lin%d" % b)
-            nc.scalar.activation(out=lin[:], in_=p_sb[:, bank_cols(b)], func=ACT.Copy, scale=lin_coef[:, b : b + 1])
+            nc.scalar.activation(out=lin[:], in_=p_bank[:, bank_cols(b)], func=ACT.Copy, scale=lin_coef[:, b : b + 1])
             add_turned(b, lin, True)
 
-        def store(b, dense, cols):
-            res = sb.tile([P, cols.stop - cols.start], F32, name="res%d" % cols.start)
-            first = b * BANK
-            nc.vector.tensor_tensor(out=res[:], in0=dense[:, cols.start - first : cols.stop - first], in1=placed[:, cols], op=ALU.add)
-            nc.sync.dma_start(out=out[:, cols], in_=res[:])
+        def store(b, dense, first, stop):
+            cols = slice(b * BANK + first, b * BANK + stop)
+            result = sb.tile([P, stop - first], F32, name="result%d" % cols.start)
+            nc.vector.tensor_tensor(out=result[:], in0=dense[:, first:stop], in1=placed[:, cols], op=ALU.add)
+            nc.sync.dma_start(out=out[:, cols], in_=result[:])
 
-        with_lin = sb.tile([P, BANK], F32, name="with_lin")
+        with_linear = sb.tile([P, BANK], F32, name="with_linear")
         nc.vector.scalar_tensor_tensor(
-            out=with_lin[:], in0=p_sb[:, bank_cols(last)], scalar=lin_coef[:, last : last + 1], in1=dense_last[:], op0=ALU.mult, op1=ALU.add
+            out=with_linear[:], in0=p_bank[:, bank_cols(LAST)], scalar=lin_coef[:, LAST : LAST + 1], in1=dense_last[:],
+            op0=ALU.mult, op1=ALU.add,
         )
-        store(last, with_lin, slice(last * BANK, last * BANK + P))
-        store(last, with_lin, slice(last * BANK + P, V))
+        store(LAST, with_linear, 0, P)
+        store(LAST, with_linear, P, BANK)
 
-        for b in range(last):
+        for b in range(LAST):
             add_linear(b)
-        for b in range(last):
+        for b in range(LAST):
             dense = turn_back(turned[b], "dense%d" % b, "row%d" % b)
-            if b + 1 < last:
-                store(b, dense, bank_cols(b))
+            if b + 1 < LAST:
+                store(b, dense, 0, BANK)
             else:
-                store(b, dense, slice(b * BANK, (b + 1) * BANK - P))
-                store(b, dense, slice((b + 1) * BANK - P, (b + 1) * BANK))
+                store(b, dense, 0, BANK - P)
+                store(b, dense, BANK - P, BANK)

import math
from contextlib import ExitStack

import concourse.mybir as mybir
from concourse.masks import make_identity

D, V, Q, I = 512, 2048, 128, 512
FLOPS = 2 * D * V * Q

F32 = mybir.dt.float32
BF16 = mybir.dt.bfloat16
I32 = mybir.dt.int32
U32 = mybir.dt.uint32
U16 = mybir.dt.uint16
U8 = mybir.dt.uint8
FP8X4 = mybir.dt.float8_e4m3fn_x4
FP4X4 = mybir.dt.float4_e2m1fn_x4
ALU = mybir.AluOpType
ACT = mybir.ActivationFunctionType

P = 128
PACK = 4
QUADRANT = 32
SCALE_ROWS = D // 32
WORD_BYTES = 2
BANK = 512
BANKS = V // BANK
LAST = BANKS - 1
BLOCKS = BANK // P
GAIN = 64.0 * 2.0 * 64.0
WORD_LOADS = ((0, 1), (1, 1), (2, 2))
GUESS_SLOPE = -math.log(2.0) / 2.0**23
GUESS_OFFSET = 88.0


def tile_attend_gpfocal_heads_kernel(tc, hid, voc_words, voc_scales, mult, sw, base, offs, out):
    nc = tc.nc
    with ExitStack() as ctx:
        sb = ctx.enter_context(tc.tile_pool(name="sb", bufs=1))
        ps = ctx.enter_context(tc.psum_pool(name="ps", bufs=1))

        def col(name, n=1):
            return sb.tile([P, n], F32, name=name)

        def listed(name):
            return sb.tile([P, I], F32, name=name)

        def bank_cols(b):
            return slice(b * BANK, (b + 1) * BANK)

        def block_cols(j):
            return slice(j * P, (j + 1) * P)

        hid_raw = sb.tile([P, PACK, Q], F32, name="hid_raw")
        nc.sync.dma_start(out=hid_raw[:], in_=hid.rearrange("(p t) q -> p t q", t=PACK))
        voc_sc = sb.tile([P, V], U8, name="voc_sc", align_bytes=64)
        for r in range(PACK):
            nc.sync.dma_start(
                out=voc_sc[r:P:QUADRANT, :].bitcast(I32),
                in_=voc_scales[0, r:SCALE_ROWS:PACK, :].bitcast(I32),
            )
        bank_bytes = WORD_BYTES * BANK
        voc_w = []
        for first, count in WORD_LOADS:
            words = sb.tile([P, count * bank_bytes], U8, name="voc_w%d" % first, align_bytes=64)
            nc.sync.dma_start(
                out=words[:].bitcast(I32),
                in_=voc_words[0, :, first * bank_bytes : (first + count) * bank_bytes].bitcast(I32),
            )
            voc_w.extend(words[:, k * bank_bytes : (k + 1) * bank_bytes] for k in range(count))
        offsets = sb.tile([P, I // 16], U16, name="offsets")
        nc.sync.dma_start(offsets[:], offs)
        sw_cols = col("sw_cols", BLOCKS)
        nc.sync.dma_start(out=sw_cols[:], in_=sw.rearrange("o (p c) -> p (o c)", c=BLOCKS))
        mul_col = col("mul_col")
        nc.sync.dma_start(out=mul_col[:], in_=mult)

        placed = sb.tile([P, V], F32, name="placed")
        nc.vector.memset(placed[:], 0.0)
        ident = sb.tile([P, P], F32, name="ident")
        make_identity(nc, ident[:])

        hid_bf = sb.tile([P, Q, PACK], BF16, name="hid_bf", tag="after_quantise", align_bytes=64)
        nc.vector.tensor_copy(out=hid_bf[:], in_=hid_raw[:].rearrange("p t q -> p q t"))
        hid_codes = sb.tile([P, Q], U32, name="hid_codes", align_bytes=64)
        hid_sc = sb.tile([P, Q], U8, name="hid_sc", align_bytes=64)
        nc.vector.quantize_mx(
            out=hid_codes[:].bitcast(FP8X4), scales=hid_sc[:], in_=hid_bf[:].rearrange("p q t -> p (q t)")
        )
        base_sb = sb.tile([P, V], F32, name="base_sb", tag="after_quantise", align_bytes=64)
        nc.sync.dma_start(out=base_sb[:], in_=base)

        neg_a = sb.tile([P, V], F32, name="neg_a")
        p_bank = sb.tile([P, V], F32, name="p_bank")
        neg_max = sb.tile([P, BANKS], F32, name="neg_max", tag="after_rescale")
        z_part = col("z_part", BANKS)
        for b in range(BANKS):
            a_ps = ps.tile([P, BANK], F32, name="a_ps", tag="row%d" % b)
            nc.tensor.matmul_mx(
                out=a_ps[:],
                lhsT=hid_codes[:].bitcast(FP8X4),
                lhsT_scale=hid_sc[:],
                rhs=voc_w[b].bitcast(FP4X4),
                rhs_scale=voc_sc[:, bank_cols(b)],
                start=True,
                stop=True,
            )
            nc.vector.tensor_scalar(
                out=neg_a[:, bank_cols(b)], in0=a_ps[:], scalar1=-1.0, scalar2=None,
                op0=ALU.mult, op1=ALU.min, accum_out=neg_max[:, b : b + 1],
            )
            nc.scalar.activation(
                out=p_bank[:, bank_cols(b)], in_=neg_a[:, bank_cols(b)], func=ACT.Exp, scale=-1.0,
                bias=neg_max[:, b : b + 1], accum_out=z_part[:, b : b + 1],
            )

        sw_ps = ps.tile([P, BANK], F32, name="sw_ps", tag="row%d" % LAST)
        for c in range(BLOCKS):
            nc.tensor.transpose(sw_ps[:, block_cols(c)], sw_cols[:, c : c + 1].to_broadcast([P, P]), ident[:])
        sw_gain = listed("sw_gain")
        sw_sum = col("sw_sum")
        nc.scalar.activation(
            out=sw_gain[:].rearrange("q (p c) -> q p c", c=BLOCKS),
            in_=sw_ps[:].rearrange("q (c p) -> q p c", c=BLOCKS),
            func=ACT.Identity,
            scale=GAIN,
            accum_out=sw_sum[:],
        )

        neg_m1 = col("neg_m1")
        nc.vector.tensor_reduce(out=neg_m1[:], in_=neg_max[:], axis=mybir.AxisListType.X, op=ALU.min)
        neg_ax = listed("neg_ax")
        nc.vector.tensor_copy(out=neg_ax[:], in_=neg_a[:].indirect(offsets[:]))

        rescale = col("rescale", BANKS)
        nc.scalar.activation(out=rescale[:], in_=neg_max[:], func=ACT.Exp, scale=-1.0, bias=neg_m1[:])
        px = listed("px")
        nc.scalar.activation(out=px[:], in_=neg_ax[:], func=ACT.Exp, scale=-1.0, bias=neg_m1[:])

        z = col("z")
        z_terms = col("z_terms", BANKS)
        nc.vector.scalar_tensor_tensor(
            out=z_terms[:], in0=rescale[:], scalar=1.0, in1=z_part[:], op0=ALU.mult, op1=ALU.mult, accum_out=z[:]
        )
        neg_mul = sb.tile([P, 2], F32, name="neg_mul", tag="after_rescale")
        nc.vector.tensor_scalar(out=neg_mul[:, 0:1], in0=mul_col[:], scalar1=-1.0, scalar2=None, op0=ALU.mult)
        nc.vector.tensor_scalar(out=neg_mul[:, 1:2], in0=mul_col[:], scalar1=-0.5, scalar2=None, op0=ALU.mult)
        neg_mul_ax = listed("neg_mul_ax")
        nc.vector.tensor_scalar(out=neg_mul_ax[:], in0=neg_ax[:], scalar1=mul_col[:], scalar2=None, op0=ALU.mult)
        inv_z = col("inv_z")
        nc.vector.reciprocal(out=inv_z[:], in_=z[:])

        neg_y0_exp = col("neg_y0_exp")
        nc.vector.tensor_scalar(
            out=neg_y0_exp[:], in0=z[:].bitcast(I32), scalar1=GUESS_SLOPE, scalar2=GUESS_OFFSET - 0.5,
            op0=ALU.mult, op1=ALU.add,
        )
        neg_y0_shift = col("neg_y0_shift")
        nc.vector.tensor_scalar(
            out=neg_y0_shift[:], in0=z[:].bitcast(I32), scalar1=GUESS_SLOPE, scalar2=GUESS_OFFSET + 1.5,
            op0=ALU.mult, op1=ALU.add,
        )
        mul_z = col("mul_z")
        nc.vector.tensor_tensor(out=mul_z[:], in0=z[:], in1=mul_col[:], op=ALU.mult)
        shift0 = col("shift0")
        nc.vector.tensor_scalar(
            out=shift0[:], in0=neg_y0_shift[:], scalar1=neg_m1[:], scalar2=neg_mul[:, 0:1], op0=ALU.add, op1=ALU.mult
        )
        to_neg_share = col("to_neg_share", BANKS)
        nc.vector.tensor_scalar(
            out=to_neg_share[:], in0=rescale[:], scalar1=inv_z[:], scalar2=-1.0, op0=ALU.mult, op1=ALU.mult
        )

        exp0 = col("exp0")
        square0 = col("square0")
        exp1 = sb.tile([P, 1], F32, name="exp1", tag="after_ln")
        shift1 = col("shift1")
        shift = col("shift")
        nc.scalar.activation(out=exp0[:], in_=z[:].bitcast(U32), func=ACT.Exp, scale=GUESS_SLOPE, bias=GUESS_OFFSET)
        nc.scalar.activation(out=square0[:], in_=exp0[:], func=ACT.Square, scale=z[:], bias=-2.0)
        nc.scalar.activation(out=exp1[:], in_=square0[:], func=ACT.Exp, scale=0.5, bias=neg_y0_exp[:])
        nc.scalar.activation(out=shift1[:], in_=square0[:], func=ACT.Identity, scale=neg_mul[:, 1:2], bias=shift0[:])
        nc.scalar.activation(out=shift[:], in_=exp1[:], func=ACT.Identity, scale=mul_z[:], bias=shift1[:])

        us = listed("us")
        us_sum = col("us_sum")
        nc.vector.scalar_tensor_tensor(
            out=us[:], in0=px[:], scalar=inv_z[:], in1=sw_gain[:], op0=ALU.mult, op1=ALU.mult, accum_out=us_sum[:]
        )
        focal = listed("focal")
        focal_sum = col("focal_sum")
        nc.vector.scalar_tensor_tensor(
            out=focal[:], in0=neg_mul_ax[:], scalar=shift[:], in1=us[:], op0=ALU.add, op1=ALU.mult,
            accum_out=focal_sum[:],
        )
        nc.vector.tensor_tensor(out=placed[:].indirect(offsets[:]), in0=focal[:], in1=sw_gain[:], op=ALU.add)

        gain_e = col("gain_e")
        nc.scalar.activation(out=gain_e[:], in_=focal_sum[:], func=ACT.Identity, bias=sw_sum[:])
        hda_coef = sb.tile([P, LAST], F32, name="hda_coef", tag="after_hda")
        nc.scalar.activation(out=hda_coef[:], in_=to_neg_share[:, 0:LAST], func=ACT.Copy, scale=gain_e[:])
        hda_coef_last = col("hda_coef_last")
        nc.scalar.activation(out=hda_coef_last[:], in_=to_neg_share[:, LAST:BANKS], func=ACT.Copy, scale=gain_e[:])
        root_e = col("root_e")
        nc.scalar.activation(out=root_e[:], in_=gain_e[:], func=ACT.Copy, scale=1.0 / math.sqrt(GAIN))
        root_coef = sb.tile([P, BANKS], F32, name="root_coef", tag="after_quads")
        nc.scalar.activation(out=root_coef[:], in_=to_neg_share[:], func=ACT.Copy, scale=root_e[:])
        neg_e = sb.tile([P, 1], F32, name="neg_e", tag="after_cross")
        nc.scalar.activation(out=neg_e[:], in_=gain_e[:], func=ACT.Copy, scale=-1.0 / GAIN)

        u_focal = listed("u_focal")
        u_focal_sum = col("u_focal_sum")
        nc.vector.scalar_tensor_tensor(
            out=u_focal[:], in0=px[:], scalar=inv_z[:], in1=focal[:], op0=ALU.mult, op1=ALU.mult,
            accum_out=u_focal_sum[:],
        )

        hda = sb.tile([P, V], F32, name="hda")
        for b in range(BANKS):
            nc.vector.scalar_tensor_tensor(
                out=hda[:, bank_cols(b)], in0=p_bank[:, bank_cols(b)], scalar=hda_coef[:, b : b + 1] if b < LAST else hda_coef_last[:],
                in1=placed[:, bank_cols(b)], op0=ALU.mult, op1=ALU.add,
            )
        gain_f = sb.tile([P, I], F32, name="gain_f", tag="after_hda")
        nc.vector.scalar_tensor_tensor(
            out=gain_f[:], in0=us[:], scalar=neg_mul[:, 0:1], in1=focal[:], op0=ALU.mult, op1=ALU.add
        )
        he_over_gain = listed("he_over_gain")
        nc.vector.tensor_scalar(
            out=he_over_gain[:], in0=hda[:].indirect(offsets[:]), scalar1=1.0 / GAIN, scalar2=0.0,
            op0=ALU.mult, op1=ALU.add,
        )

        turned = []
        for b in range(BANKS):
            bank_sum = ps.tile([P, BANK], F32, name="bank_sum", tag="turned%d" % b)
            turned.append(bank_sum)
            for j in range(BLOCKS):
                nc.tensor.matmul(
                    bank_sum[:, block_cols(j)], base_sb[:, block_cols(b * BLOCKS + j)], ident[:],
                    start=(j == 0), stop=False, is_transpose=True,
                )

        def add_turned(b, term, closes):
            for j in range(BLOCKS):
                nc.tensor.matmul(
                    turned[b][:, block_cols(j)], term[:, block_cols(j)], ident[:],
                    start=False, stop=(closes and j == BLOCKS - 1), is_transpose=True,
                )

        def turn_back(total, name, tag):
            staged = sb.tile([P, BANK], F32, name=name + "_staged")
            nc.scalar.copy(out=staged[:], in_=total[:])
            back = ps.tile([P, BANK], F32, name=name, tag=tag)
            for j in range(BLOCKS):
                nc.tensor.transpose(back[:, block_cols(j)], staged[:, block_cols(j)], ident[:])
            return back

        def add_quadratic(b):
            quad = sb.tile([P, BANK], F32, name="quad%d" % b)
            nc.scalar.activation(
                out=quad[:], in_=p_bank[:, bank_cols(b)], func=ACT.Square, scale=root_coef[:, b : b + 1]
            )
            add_turned(b, quad, b == LAST)

        add_quadratic(LAST)
        dense_last = turn_back(turned[LAST], "dense_last", "row%d" % LAST)
        for b in range(LAST):
            add_quadratic(b)

        sq_part = col("sq_part", BANKS)
        squares = [
            sb.tile([P, BANK], BF16, name="squares_early", tag="after_ln"),
            sb.tile([P, BANK], BF16, name="squares_late", tag="after_quads"),
        ]
        for b in range(BANKS):
            nc.scalar.activation(
                out=squares[b // 2][:], in_=p_bank[:, bank_cols(b)], func=ACT.Square,
                scale=to_neg_share[:, b : b + 1], accum_out=sq_part[:, b : b + 1],
            )
        gain_sq_sum = col("gain_sq_sum")
        sq_terms = col("sq_terms", BANKS)
        nc.scalar.activation(out=sq_terms[:], in_=sq_part[:], func=ACT.Identity, scale=GAIN, accum_out=gain_sq_sum[:])

        g_part = col("g_part")
        nc.scalar.activation(out=g_part[:], in_=gain_sq_sum[:], func=ACT.Identity, scale=neg_e[:], bias=us_sum[:])
        g = col("g")
        nc.scalar.activation(out=g[:], in_=u_focal_sum[:], func=ACT.Identity, bias=g_part[:])
        g_over_gain = col("g_over_gain")
        nc.scalar.activation(out=g_over_gain[:], in_=g[:], func=ACT.Copy, scale=1.0 / GAIN)
        neg_ge = col("neg_ge")
        nc.scalar.activation(out=neg_ge[:], in_=g[:], func=ACT.Copy, scale=neg_e[:])
        lin_early = col("lin_early", BANKS)
        nc.scalar.activation(out=lin_early[:], in_=to_neg_share[:], func=ACT.Copy, scale=neg_ge[:])

        ue_turned = ps.tile([P, I], F32, name="ue_turned", tag="turned%d" % LAST)
        for j in range(BLOCKS):
            for term, opens in ((us, True), (u_focal, False)):
                nc.tensor.matmul(
                    ue_turned[:, block_cols(j)], term[:, block_cols(j)], ident[:],
                    start=opens, stop=not opens, is_transpose=True,
                )
        ue = turn_back(ue_turned, "ue", "row0")
        cross = listed("cross")
        nc.scalar.activation(out=cross[:], in_=ue[:], func=ACT.Copy, scale=neg_e[:])

        e51 = listed("e51")
        e51_sum = col("e51_sum")
        nc.vector.scalar_tensor_tensor(
            out=e51[:], in0=he_over_gain[:], scalar=g_over_gain[:], in1=gain_f[:], op0=ALU.subtract, op1=ALU.mult,
            accum_out=e51_sum[:],
        )
        nc.vector.tensor_tensor(out=placed[:].indirect(offsets[:]), in0=e51[:], in1=cross[:], op=ALU.add)

        lin_coef = sb.tile([P, BANKS], F32, name="lin_coef", tag="after_cross")
        for b in range(BANKS):
            nc.scalar.activation(
                out=lin_coef[:, b : b + 1], in_=e51_sum[:], func=ACT.Identity,
                scale=to_neg_share[:, b : b + 1], bias=lin_early[:, b : b + 1],
            )

        def add_linear(b):
            lin = sb.tile([P, BANK], F32, name="lin%d" % b)
            nc.scalar.activation(out=lin[:], in_=p_bank[:, bank_cols(b)], func=ACT.Copy, scale=lin_coef[:, b : b + 1])
            add_turned(b, lin, True)

        def store(b, dense, first, stop):
            cols = slice(b * BANK + first, b * BANK + stop)
            result = sb.tile([P, stop - first], F32, name="result%d" % cols.start)
            nc.vector.tensor_tensor(out=result[:], in0=dense[:, first:stop], in1=placed[:, cols], op=ALU.add)
            nc.sync.dma_start(out=out[:, cols], in_=result[:])

        with_linear = sb.tile([P, BANK], F32, name="with_linear")
        nc.vector.scalar_tensor_tensor(
            out=with_linear[:], in0=p_bank[:, bank_cols(LAST)], scalar=lin_coef[:, LAST : LAST + 1], in1=dense_last[:],
            op0=ALU.mult, op1=ALU.add,
        )
        store(LAST, with_linear, 0, P)
        store(LAST, with_linear, P, BANK)

        for b in range(LAST):
            add_linear(b)
        for b in range(LAST):
            dense = turn_back(turned[b], "dense%d" % b, "row%d" % b)
            if b + 1 < LAST:
                store(b, dense, 0, BANK)
            else:
                store(b, dense, 0, BANK - P)
                store(b, dense, BANK - P, BANK)
